import numpy as np
import ml_dtypes


def mxq(x, axis, fmt="e4m3"):
    dtype, down = {"e4m3": (ml_dtypes.float8_e4m3fn, 7), "e5m2": (ml_dtypes.float8_e5m2, 14)}[fmt]
    v = np.moveaxis(np.asarray(x, np.float32).astype(ml_dtypes.bfloat16).astype(np.float64), axis, -1)
    blocks = v.reshape(v.shape[:-1] + (-1, 32))
    amax = np.abs(blocks).max(-1, keepdims=True)
    byte = np.maximum(np.where(amax > 0, np.frexp(amax)[1] - 1 + 127, 0) - down, 1)
    scale = np.exp2(byte - 127.0)
    codes = (blocks / scale).astype(np.float32).astype(dtype).astype(np.float64)
    return np.moveaxis((codes * scale).reshape(v.shape), -1, axis)


WIDE = False


def mx_kscale(k):
    if not WIDE:
        return np.ones(k)
    levels = np.array([10, -10, 5, -5, 0])
    if k % 512:
        return np.exp2(np.random.permutation(np.resize(levels, k // 32))).repeat(32)
    a = np.empty((k // 512, 16))
    for p in range(k // 512):
        a[p, :8] = np.random.permutation(np.resize(levels, 8))
        for g in range(8):
            far = levels[np.abs(levels - a[p, g]) >= 10]
            a[p, g + 8] = far[np.random.randint(len(far))]
    return np.exp2(a.ravel()).repeat(32)


def f64(x):
    return np.asarray(x).astype(np.float64)


def striped(idx):
    return np.tile(idx.reshape(-1, 16).T, (8, 1)).astype(np.uint16)


def unstriped(offs):
    return offs[:16].T.reshape(-1).astype(np.int64)


def pack_weight(w):
    k, n = w.shape
    w = f64(np.asarray(w, np.float32).astype(ml_dtypes.bfloat16)).reshape(k // 32, 32, n)
    amax = np.abs(w).max(1)
    byte = np.clip(np.where(amax > 0, np.frexp(amax)[1] - 1 + 127 - 7, 1), 1, 254)
    scaled = (w * np.exp2(127.0 - byte)[:, None, :]).reshape(k, n).astype(np.float32)
    words = np.ascontiguousarray(scaled.reshape(k // 512, 128, 4, n).transpose(0, 1, 3, 2)).astype(ml_dtypes.float8_e4m3fn).view(np.uint8)
    return words, np.ascontiguousarray(byte.astype(np.uint8).reshape(k // 512, 16, n))


def unpack_weight(words, scales):
    g, p, n, _ = words.shape
    vals = np.ascontiguousarray(words).view(ml_dtypes.float8_e4m3fn).astype(np.float64) * np.repeat(np.exp2(scales.astype(np.float64) - 127.0), 8, axis=1)[..., None]
    return vals.transpose(0, 1, 3, 2).reshape(g * 512, n)


def planes(y):
    n, m = y.shape
    v = y.astype(np.float32).astype(ml_dtypes.bfloat16).astype(np.float64).reshape(n // 32, 32, m)
    top = np.abs(v).max(1)
    byte = np.clip(np.where(top > 0, np.frexp(top)[1] - 1 + 127 - 7, 1), 1, 254)
    codes = (v * np.exp2(127.0 - byte)[:, None, :]).reshape(n, m).astype(np.float32).astype(ml_dtypes.float8_e4m3fn).view(np.uint8)
    words = codes.reshape(n // 512, 128, 4, m).transpose(0, 1, 3, 2)
    return np.ascontiguousarray(words), np.ascontiguousarray(byte.astype(np.uint8).reshape(n // 512, 16, m))


def sigmoid(v):
    return 1.0 / (1.0 + np.exp(-np.maximum(v, -700.0)))


K, T, S, N = 512, 2048, 1024, 512


def setup_inputs():
    n = np.random.standard_normal
    s = mx_kscale(K)[:, None]
    packed_xT = pack_weight(n((K, T)) * s)
    return {
        "x_words": packed_xT[0],
        "x_scales": packed_xT[1],
        "w1": (n((K, N)) / np.sqrt(K) / s).astype(np.float32),
        "w2": (n((K, N)) / np.sqrt(K) / s).astype(np.float32),
        "offs": striped(np.random.permutation(T)[:S]),
    }


def reference(x_words, x_scales, w1, w2, offs):
    xq = unpack_weight(x_words, x_scales)[:, unstriped(offs)]
    y = mxq(f64(w1), 0, "e4m3").T @ xq
    a = sigmoid(mxq(f64(w2), 0, "e4m3").T @ xq)
    h = y + a * (np.pad(y, ((0, 0), (1, 0)))[:, :S])
    rr = a * (np.pad(a, ((0, 0), (1, 0)))[:, :S])
    out_0 = h + rr * (np.pad(h, ((0, 0), (2, 0)))[:, :S])
    return (out_0,) + planes(out_0)

@@ -1,0 +1,188 @@
+from contextlib import ExitStack
+
+import concourse.mybir as mybir
+
+K, T, S, N = 512, 2048, 1024, 512
+FLOPS = 2 * 2 * K * N * S
+
+F32 = mybir.dt.float32
+BF16 = mybir.dt.bfloat16
+I32 = mybir.dt.int32
+U32 = mybir.dt.uint32
+U16 = mybir.dt.uint16
+U8 = mybir.dt.uint8
+FP8X4 = mybir.dt.float8_e4m3fn_x4
+MULT = mybir.AluOpType.mult
+ADD = mybir.AluOpType.add
+SIGMOID = mybir.ActivationFunctionType.Sigmoid
+
+P = 128
+PACK = 4
+BANK = 512
+CHUNKS = S // BANK
+PAD = 8
+PIECES = (256, 256, 256, 128, 128)
+
+
+def tile_picked_yscan_free_po_kernel(
+    tc, x_words, x_scales, w1, w2, offs, out_0, out_1, out_2
+):
+    nc = tc.nc
+    with ExitStack() as ctx:
+        keep = ctx.enter_context(tc.tile_pool(name="keep", bufs=1))
+        psum = ctx.enter_context(tc.psum_pool(name="psum", bufs=4))
+
+        offsets = keep.tile([P, S // 16], U16, name="offsets")
+        nc.sync.dma_start(offsets[:], offs)
+
+        scale_table = keep.tile([P, T], U8, name="scale_table", align_bytes=64)
+        nc.vector.memset(scale_table[:].bitcast(I32), 0)
+        for q in range(4):
+            nc.scalar.dma_start(
+                scale_table[32 * q : 32 * q + 4, :].bitcast(I32),
+                x_scales[0, 4 * q : 4 * q + 4, :].bitcast(I32),
+            )
+
+        word_table = keep.tile([P, T], I32, name="word_table", align_bytes=64)
+        nc.sync.dma_start(word_table[:], x_words[0].rearrange("p n r -> p (n r)").bitcast(I32))
+
+        raw2 = keep.tile([P, PACK, N], F32, name="raw2", align_bytes=64)
+        nc.sync.dma_start(raw2[:], w2.rearrange("(p j) c -> p j c", j=PACK))
+        raw1 = keep.tile([P, PACK, N], F32, name="raw1", align_bytes=64)
+        nc.sync.dma_start(raw1[:], w1.rearrange("(p j) c -> p j c", j=PACK))
+
+        gate = keep.tile([P, PACK, PAD + S], F32, name="gate", align_bytes=64)
+        step1 = keep.tile([P, PACK, PAD + S], F32, name="step1", align_bytes=64)
+        h = keep.tile([P, PACK, PAD + S], F32, name="h", align_bytes=64)
+        rr = keep.tile([P, PACK, S], F32, name="rr", align_bytes=64)
+        nc.vector.memset(step1[:, :, 0:PAD], 0.0)
+        nc.vector.memset(h[:, :, 0:PAD], 0.0)
+        nc.scalar.activation(gate[:, :, 0:PAD], h[:, :, 0:PAD], SIGMOID)
+
+        x_codes, x_bytes = [], []
+        for c in range(CHUNKS):
+            picked = offsets[:, c * BANK // 16 : (c + 1) * BANK // 16]
+            sc = keep.tile([P, BANK], U8, name=f"x_bytes{c}", align_bytes=64)
+            nc.vector.tensor_copy(sc[:], scale_table[:].indirect(picked))
+            x_bytes.append(sc)
+        for c in range(CHUNKS):
+            picked = offsets[:, c * BANK // 16 : (c + 1) * BANK // 16]
+            co = keep.tile([P, BANK], U32, name=f"x_codes{c}", align_bytes=64)
+            nc.vector.tensor_copy(co[:], word_table[:].bitcast(U32).indirect(picked))
+            x_codes.append(co)
+
+        def deal(copy, raw, name):
+            grouped = keep.tile([P, PACK, P, PACK], BF16, name=f"grouped{name}", align_bytes=64)
+            copy(
+                grouped[:].rearrange("p t m j -> p m j t"),
+                raw[:].rearrange("p j (m t) -> p m j t", t=PACK),
+            )
+            return grouped
+
+        def quantise(grouped, name):
+            codes = keep.tile([P, N], U32, name=f"w_codes{name}", align_bytes=64)
+            scales = keep.tile([P, N], U8, name=f"w_scales{name}", align_bytes=64)
+            nc.vector.quantize_mx(
+                out=codes[:].bitcast(FP8X4),
+                scales=scales[:],
+                in_=grouped[:].rearrange("p t m j -> p (t m j)"),
+            )
+            return codes, scales
+
+        def product(weights, t, c, tag):
+            codes, scales = weights
+            acc = psum.tile([P, BANK], F32, name=tag)
+            nc.tensor.matmul_mx(
+                out=acc[:],
+                lhsT=codes[:, t * P : (t + 1) * P].bitcast(FP8X4),
+                lhsT_scale=scales[:, t * P : (t + 1) * P],
+                rhs=x_codes[c][:].bitcast(FP8X4),
+                rhs_scale=x_bytes[c][:],
+                start=True,
+                stop=True,
+            )
+            return acc
+
+        q2 = quantise(deal(nc.scalar.copy, raw2, "2"), "2")
+        q1 = quantise(deal(nc.vector.tensor_copy, raw1, "1"), "1")
+
+        for t in range(PACK):
+            for c in range(CHUNKS):
+                u = product(q2, t, c, "u")
+                nc.scalar.activation(gate[:, t, PAD + c * BANK : PAD + (c + 1) * BANK], u[:], SIGMOID)
+            for c in range(CHUNKS):
+                lo = c * BANK
+                nc.gpsimd.tensor_tensor(
+                    rr[:, t, lo : lo + BANK],
+                    gate[:, t, PAD + lo : PAD + lo + BANK],
+                    gate[:, t, PAD + lo - 1 : PAD + lo + BANK - 1],
+                    MULT,
+                )
+        for t in range(PACK):
+            y = [product(q1, t, c, "y") for c in range(CHUNKS)]
+            for c in range(CHUNKS):
+                lo = c * BANK
+                n = min(BANK, S - 1 - lo)
+                nc.vector.tensor_tensor(
+                    step1[:, t, PAD + lo : PAD + lo + n],
+                    y[c][:, 0:n],
+                    gate[:, t, PAD + lo + 1 : PAD + lo + 1 + n],
+                    MULT,
+                )
+            for c in range(CHUNKS):
+                lo = c * BANK
+                nc.vector.tensor_tensor(
+                    h[:, t, PAD + lo : PAD + lo + BANK],
+                    y[c][:],
+                    step1[:, t, PAD + lo - 1 : PAD + lo + BANK - 1],
+                    ADD,
+                )
+
+        out_words = keep.tile([P, S], U32, name="out_words", align_bytes=64)
+        out_scales = keep.tile([P, S], U8, name="out_scales", align_bytes=64)
+        out_rows = out_0.rearrange("(p t) s -> p t s", t=PACK)
+        words_hbm = out_1[0].rearrange("p n r -> p (n r)").bitcast(I32)
+        starts = [sum(PIECES[:i]) for i in range(len(PIECES))]
+        step2, rounded = {}, {}
+
+        def second_product(i):
+            lo, w = starts[i], PIECES[i]
+            step2[i] = keep.tile([P, PACK, w], F32, name=f"step2_{i}", align_bytes=64)
+            nc.vector.tensor_tensor(
+                step2[i][:], rr[:, :, lo : lo + w], h[:, :, PAD + lo - 2 : PAD + lo - 2 + w], MULT
+            )
+
+        def finish(i):
+            lo, w = starts[i], PIECES[i]
+            result = keep.tile([P, PACK, w], F32, name=f"result{i}", align_bytes=64)
+            nc.vector.tensor_tensor(result[:], step2[i][:], h[:, :, PAD + lo : PAD + lo + w], ADD)
+            nc.sync.dma_start(out_rows[:, :, lo : lo + w], result[:])
+            rounded[i] = keep.tile([P, w, PACK], BF16, name=f"rounded{i}", align_bytes=64)
+            nc.scalar.copy(
+                rounded[i][:].rearrange("p (c i) t -> p c t i", i=4),
+                result[:].rearrange("p t (c i) -> p c t i", i=4),
+            )
+
+        def hand_on(i):
+            lo, w = starts[i], PIECES[i]
+            nc.vector.quantize_mx(
+                out=out_words[:, lo : lo + w].bitcast(FP8X4),
+                scales=out_scales[:, lo : lo + w],
+                in_=rounded[i][:].rearrange("p n t -> p (n t)"),
+            )
+            nc.sync.dma_start(words_hbm[:, lo : lo + w], out_words[:, lo : lo + w].bitcast(I32))
+
+        last = len(PIECES) - 1
+        second_product(0)
+        for i in range(len(PIECES)):
+            if i < last:
+                second_product(i + 1)
+            finish(i)
+            if i >= 1:
+                hand_on(i - 1)
+        hand_on(last)
+        for q in range(4):
+            nc.scalar.dma_start(
+                out_2[0, 4 * q : 4 * q + 4, :].bitcast(I32),
+                out_scales[32 * q : 32 * q + 4, :].bitcast(I32),
+            )

@@ -1,6 +1,7 @@
 from contextlib import ExitStack
 
 import concourse.mybir as mybir
+from concourse.masks import make_identity
 
 K, T, S, N = 512, 2048, 1024, 512
 FLOPS = 2 * 2 * K * N * S
@@ -18,10 +19,13 @@ SIGMOID = mybir.ActivationFunctionType.Sigmoid
 
 P = 128
 PACK = 4
-BANK = 512
-CHUNKS = S // BANK
+UNIT = 128
+UNITS = S // UNIT
+GATHER = 256
 PAD = 8
-PIECES = (256, 256, 256, 128, 128)
+ROUNDS = (2, 3, 3)
+ON_TENSOR = 5
+WORD_STORES = (5, 8)
 
 
 def tile_picked_yscan_free_po_kernel(
@@ -30,58 +34,55 @@ def tile_picked_yscan_free_po_kernel(
     nc = tc.nc
     with ExitStack() as ctx:
         keep = ctx.enter_context(tc.tile_pool(name="keep", bufs=1))
+        loads = ctx.enter_context(tc.tile_pool(name="loads", bufs=1))
+        ring = ctx.enter_context(tc.tile_pool(name="ring", bufs=1))
         psum = ctx.enter_context(tc.psum_pool(name="psum", bufs=4))
 
         offsets = keep.tile([P, S // 16], U16, name="offsets")
         nc.sync.dma_start(offsets[:], offs)
 
-        scale_table = keep.tile([P, T], U8, name="scale_table", align_bytes=64)
+        raw2 = keep.tile([P, PACK, N], F32, name="raw2", align_bytes=64)
+        nc.sync.dma_start(raw2[:], w2.rearrange("(p j) c -> p j c", j=PACK))
+
+        scale_table = loads.tile([P, T], U8, name="scale_table", offset=16384, align_bytes=64)
         nc.vector.memset(scale_table[:].bitcast(I32), 0)
         for q in range(4):
-            nc.scalar.dma_start(
+            nc.sync.dma_start(
                 scale_table[32 * q : 32 * q + 4, :].bitcast(I32),
                 x_scales[0, 4 * q : 4 * q + 4, :].bitcast(I32),
             )
 
-        word_table = keep.tile([P, T], I32, name="word_table", align_bytes=64)
-        nc.sync.dma_start(word_table[:], x_words[0].rearrange("p n r -> p (n r)").bitcast(I32))
-
-        raw2 = keep.tile([P, PACK, N], F32, name="raw2", align_bytes=64)
-        nc.sync.dma_start(raw2[:], w2.rearrange("(p j) c -> p j c", j=PACK))
-        raw1 = keep.tile([P, PACK, N], F32, name="raw1", align_bytes=64)
-        nc.sync.dma_start(raw1[:], w1.rearrange("(p j) c -> p j c", j=PACK))
-
         gate = keep.tile([P, PACK, PAD + S], F32, name="gate", align_bytes=64)
-        step1 = keep.tile([P, PACK, PAD + S], F32, name="step1", align_bytes=64)
-        h = keep.tile([P, PACK, PAD + S], F32, name="h", align_bytes=64)
-        rr = keep.tile([P, PACK, S], F32, name="rr", align_bytes=64)
-        nc.vector.memset(step1[:, :, 0:PAD], 0.0)
-        nc.vector.memset(h[:, :, 0:PAD], 0.0)
+        both = keep.tile([P, 2 * PACK, PAD + S], F32, name="both", align_bytes=64)
+        step1 = both[:, 0:PACK, :]
+        h = both[:, PACK : 2 * PACK, :]
+        zeros = loads.tile([P, T + PACK * N], F32, name="zeros", offset=0, align_bytes=64)
+        nc.vector.memset(zeros[:, 0 : 2 * PACK * PAD], 0.0)
+        nc.vector.tensor_copy(
+            both[:, :, 0:PAD], zeros[:, 0 : 2 * PACK * PAD].rearrange("p (r c) -> p r c", c=PAD)
+        )
         nc.scalar.activation(gate[:, :, 0:PAD], h[:, :, 0:PAD], SIGMOID)
 
-        x_codes, x_bytes = [], []
-        for c in range(CHUNKS):
-            picked = offsets[:, c * BANK // 16 : (c + 1) * BANK // 16]
-            sc = keep.tile([P, BANK], U8, name=f"x_bytes{c}", align_bytes=64)
-            nc.vector.tensor_copy(sc[:], scale_table[:].indirect(picked))
-            x_bytes.append(sc)
-        for c in range(CHUNKS):
-            picked = offsets[:, c * BANK // 16 : (c + 1) * BANK // 16]
-            co = keep.tile([P, BANK], U32, name=f"x_codes{c}", align_bytes=64)
-            nc.vector.tensor_copy(co[:], word_table[:].bitcast(U32).indirect(picked))
-            x_codes.append(co)
+        raw1 = loads.tile([P, PACK, N], F32, name="raw1", offset=4 * T, align_bytes=64)
+        nc.sync.dma_start(raw1[:], w1.rearrange("(p j) c -> p j c", j=PACK))
+        word_table = loads.tile([P, T], I32, name="word_table", offset=0, align_bytes=64)
+        nc.sync.dma_start(word_table[:], x_words[0].rearrange("p n r -> p (n r)").bitcast(I32))
 
-        def deal(copy, raw, name):
+        identity = keep.tile([P, P], F32, name="identity", align_bytes=64)
+        make_identity(nc, identity[:])
+
+        def deal(raw, name, scalar_share):
             grouped = keep.tile([P, PACK, P, PACK], BF16, name=f"grouped{name}", align_bytes=64)
-            copy(
-                grouped[:].rearrange("p t m j -> p m j t"),
-                raw[:].rearrange("p j (m t) -> p m j t", t=PACK),
-            )
+            dealt = grouped[:].rearrange("p t m j -> p m j t")
+            source = raw[:].rearrange("p j (m t) -> p m j t", t=PACK)
+            nc.scalar.copy(dealt[:, 0:scalar_share], source[:, 0:scalar_share])
+            if scalar_share < P:
+                nc.vector.tensor_copy(dealt[:, scalar_share:P], source[:, scalar_share:P])
             return grouped
 
-        def quantise(grouped, name):
+        def quantise(grouped, name, place):
             codes = keep.tile([P, N], U32, name=f"w_codes{name}", align_bytes=64)
-            scales = keep.tile([P, N], U8, name=f"w_scales{name}", align_bytes=64)
+            scales = loads.tile([P, N], U8, name=f"w_scales{name}", offset=16384 + place * N, align_bytes=64)
             nc.vector.quantize_mx(
                 out=codes[:].bitcast(FP8X4),
                 scales=scales[:],
@@ -89,100 +90,178 @@ def tile_picked_yscan_free_po_kernel(
             )
             return codes, scales
 
-        def product(weights, t, c, tag):
+        grouped2 = deal(raw2, "2", P)
+        x_bytes = keep.tile([P, S], U8, name="x_bytes", align_bytes=64)
+        nc.vector.tensor_copy(x_bytes[:], scale_table[:].indirect(offsets[:]))
+        q2 = quantise(grouped2, "2", 0)
+        q1 = quantise(deal(raw1, "1", P // 2), "1", 1)
+
+        x_codes = []
+        for c in range(S // GATHER):
+            picked = offsets[:, c * GATHER // 16 : (c + 1) * GATHER // 16]
+            codes = keep.tile([P, GATHER], U32, name=f"x_codes{c}", align_bytes=64)
+            nc.vector.tensor_copy(codes[:], word_table[:].bitcast(U32).indirect(picked))
+            x_codes.append(codes)
+
+        def product(weights, u, tag):
             codes, scales = weights
-            acc = psum.tile([P, BANK], F32, name=tag)
-            nc.tensor.matmul_mx(
-                out=acc[:],
-                lhsT=codes[:, t * P : (t + 1) * P].bitcast(FP8X4),
-                lhsT_scale=scales[:, t * P : (t + 1) * P],
-                rhs=x_codes[c][:].bitcast(FP8X4),
-                rhs_scale=x_bytes[c][:],
-                start=True,
-                stop=True,
-            )
+            acc = psum.tile([P, PACK, UNIT], F32, name=tag)
+            c, lo = divmod(u * UNIT, GATHER)
+            for t in range(PACK):
+                nc.tensor.matmul_mx(
+                    out=acc[:, t, :],
+                    lhsT=codes[:, t * P : (t + 1) * P].bitcast(FP8X4),
+                    lhsT_scale=scales[:, t * P : (t + 1) * P],
+                    rhs=x_codes[c][:, lo : lo + UNIT].bitcast(FP8X4),
+                    rhs_scale=x_bytes[:, u * UNIT : (u + 1) * UNIT],
+                    start=True,
+                    stop=True,
+                )
             return acc
 
-        q2 = quantise(deal(nc.scalar.copy, raw2, "2"), "2")
-        q1 = quantise(deal(nc.vector.tensor_copy, raw1, "1"), "1")
+        y = {}
 
-        for t in range(PACK):
-            for c in range(CHUNKS):
-                u = product(q2, t, c, "u")
-                nc.scalar.activation(gate[:, t, PAD + c * BANK : PAD + (c + 1) * BANK], u[:], SIGMOID)
-            for c in range(CHUNKS):
-                lo = c * BANK
-                nc.gpsimd.tensor_tensor(
-                    rr[:, t, lo : lo + BANK],
-                    gate[:, t, PAD + lo : PAD + lo + BANK],
-                    gate[:, t, PAD + lo - 1 : PAD + lo + BANK - 1],
-                    MULT,
-                )
-        for t in range(PACK):
-            y = [product(q1, t, c, "y") for c in range(CHUNKS)]
-            for c in range(CHUNKS):
-                lo = c * BANK
-                n = min(BANK, S - 1 - lo)
-                nc.vector.tensor_tensor(
-                    step1[:, t, PAD + lo : PAD + lo + n],
-                    y[c][:, 0:n],
-                    gate[:, t, PAD + lo + 1 : PAD + lo + 1 + n],
-                    MULT,
-                )
-            for c in range(CHUNKS):
-                lo = c * BANK
-                nc.vector.tensor_tensor(
-                    h[:, t, PAD + lo : PAD + lo + BANK],
-                    y[c][:],
-                    step1[:, t, PAD + lo - 1 : PAD + lo + BANK - 1],
-                    ADD,
-                )
+        def gates(u):
+            acc = product(q2, u, "stage")
+            nc.scalar.activation(gate[:, :, PAD + u * UNIT : PAD + (u + 1) * UNIT], acc[:], SIGMOID)
 
-        out_words = keep.tile([P, S], U32, name="out_words", align_bytes=64)
+        def first_product(u):
+            lo = u * UNIT
+            n = min(UNIT, S - 1 - lo)
+            nc.vector.tensor_tensor(
+                step1[:, :, PAD + lo : PAD + lo + n],
+                gate[:, :, PAD + lo + 1 : PAD + lo + 1 + n],
+                y[u][:, :, 0:n],
+                MULT,
+            )
+
+        def first_sum(u):
+            lo = u * UNIT
+            nc.vector.tensor_tensor(
+                h[:, :, PAD + lo : PAD + lo + UNIT],
+                step1[:, :, PAD + lo - 1 : PAD + lo + UNIT - 1],
+                y[u][:],
+                ADD,
+            )
+
+        out_words = loads.tile([P, S], U32, name="out_words", offset=0, align_bytes=64)
         out_scales = keep.tile([P, S], U8, name="out_scales", align_bytes=64)
         out_rows = out_0.rearrange("(p t) s -> p t s", t=PACK)
         words_hbm = out_1[0].rearrange("p n r -> p (n r)").bitcast(I32)
-        starts = [sum(PIECES[:i]) for i in range(len(PIECES))]
-        step2, rounded = {}, {}
+        step2, rounded, sums = {}, {}, {}
 
-        def second_product(i):
-            lo, w = starts[i], PIECES[i]
-            step2[i] = keep.tile([P, PACK, w], F32, name=f"step2_{i}", align_bytes=64)
+        def second_product(u, rr, first):
+            lo = u * UNIT
+            step2[u] = keep.tile([P, PACK, UNIT], F32, name=f"step2_{u}", align_bytes=64)
             nc.vector.tensor_tensor(
-                step2[i][:], rr[:, :, lo : lo + w], h[:, :, PAD + lo - 2 : PAD + lo - 2 + w], MULT
+                step2[u][:],
+                rr[:, :, (u - first) * UNIT : (u - first + 1) * UNIT],
+                h[:, :, PAD + lo - 2 : PAD + lo - 2 + UNIT],
+                MULT,
             )
 
-        def finish(i):
-            lo, w = starts[i], PIECES[i]
-            result = keep.tile([P, PACK, w], F32, name=f"result{i}", align_bytes=64)
-            nc.vector.tensor_tensor(result[:], step2[i][:], h[:, :, PAD + lo : PAD + lo + w], ADD)
-            nc.sync.dma_start(out_rows[:, :, lo : lo + w], result[:])
-            rounded[i] = keep.tile([P, w, PACK], BF16, name=f"rounded{i}", align_bytes=64)
+        def second_sum_on_tensor(u):
+            lo = u * UNIT
+            turned = psum.tile([P, PACK, P], F32, name="stage")
+            for t in range(PACK):
+                nc.tensor.matmul(
+                    turned[:, t, :], h[:, t, PAD + lo : PAD + lo + UNIT], identity[:],
+                    start=True, stop=False, is_transpose=True,
+                )
+                nc.tensor.matmul(
+                    turned[:, t, :], step2[u][:, t, :], identity[:],
+                    start=False, stop=True, is_transpose=True,
+                )
+            by_token = ring.tile(
+                [P, PACK, P], F32, name=f"by_token{u}", align_bytes=64,
+                offset=512 if (ON_TENSOR - 1 - u) % 2 == 0 else 4096,
+            )
+            nc.scalar.copy(by_token[:], turned[:])
+            sums[u] = by_token
+
+        def turn_back(u):
+            lo = u * UNIT
+            by_token = sums[u]
+            back = psum.tile([P, PACK, UNIT], F32, name="stage")
+            for t in range(PACK):
+                nc.tensor.transpose(back[:, t, :], by_token[:, t, :], identity[:])
+            result = keep.tile([P, PACK, UNIT], F32, name=f"result{u}", align_bytes=64)
+            nc.scalar.copy(result[:], back[:])
+            nc.sync.dma_start(out_rows[:, :, lo : lo + UNIT], result[:])
+            rounded[u] = keep.tile([P, UNIT, PACK], BF16, name=f"rounded{u}", align_bytes=64)
+            nc.scalar.copy(rounded[u][:], back[:].rearrange("p t n -> p n t"))
+
+        def second_sum_on_vector(u):
+            lo = u * UNIT
+            result = keep.tile([P, PACK, UNIT], F32, name=f"result{u}", align_bytes=64)
+            nc.vector.tensor_tensor(result[:], step2[u][:], h[:, :, PAD + lo : PAD + lo + UNIT], ADD)
+            nc.sync.dma_start(out_rows[:, :, lo : lo + UNIT], result[:])
+            rounded[u] = ring.tile(
+                [P, UNIT, PACK], BF16, name=f"rounded{u}", align_bytes=64, offset=1024 * (u - ON_TENSOR)
+            )
             nc.scalar.copy(
-                rounded[i][:].rearrange("p (c i) t -> p c t i", i=4),
+                rounded[u][:].rearrange("p (c i) t -> p c t i", i=4),
                 result[:].rearrange("p t (c i) -> p c t i", i=4),
             )
 
-        def hand_on(i):
-            lo, w = starts[i], PIECES[i]
+        def hand_on(u):
+            lo = u * UNIT
             nc.vector.quantize_mx(
-                out=out_words[:, lo : lo + w].bitcast(FP8X4),
-                scales=out_scales[:, lo : lo + w],
-                in_=rounded[i][:].rearrange("p n t -> p (n t)"),
+                out=out_words[:, lo : lo + UNIT].bitcast(FP8X4),
+                scales=out_scales[:, lo : lo + UNIT],
+                in_=rounded[u][:].rearrange("p n t -> p (n t)"),
             )
-            nc.sync.dma_start(words_hbm[:, lo : lo + w], out_words[:, lo : lo + w].bitcast(I32))
+            if u + 1 in WORD_STORES:
+                before = max(e for e in (0,) + WORD_STORES if e <= u) * UNIT
+                nc.sync.dma_start(
+                    words_hbm[:, before : lo + UNIT], out_words[:, before : lo + UNIT].bitcast(I32)
+                )
 
-        last = len(PIECES) - 1
-        second_product(0)
-        for i in range(len(PIECES)):
-            if i < last:
-                second_product(i + 1)
-            finish(i)
-            if i >= 1:
-                hand_on(i - 1)
-        hand_on(last)
+        gates(0)
+        for u in range(UNITS):
+            if u + 1 < UNITS:
+                gates(u + 1)
+            if u < 4:
+                y[u] = product(q1, u, "y")
+
+        places = max(count + i for i, count in enumerate(ROUNDS))
+        rr_all = loads.tile([P, PACK, places * UNIT], F32, name="rr_all", offset=0, align_bytes=64)
+        first = 0
+        for count in ROUNDS:
+            units = range(first, first + count)
+            lo = first * UNIT
+            rr = rr_all[:, :, (places - count) * UNIT : places * UNIT]
+            places = places - 1
+            nc.gpsimd.tensor_tensor(
+                rr,
+                gate[:, :, PAD + lo : PAD + lo + count * UNIT],
+                gate[:, :, PAD + lo - 1 : PAD + lo - 1 + count * UNIT],
+                MULT,
+            )
+            for u in units:
+                first_product(u)
+                if u > first:
+                    first_sum(u - 1)
+            first_sum(units[-1])
+            for u in units:
+                if u + 4 < UNITS:
+                    y[u + 4] = product(q1, u + 4, "y")
+            for u in units:
+                second_product(u, rr, first)
+                if u < ON_TENSOR:
+                    second_sum_on_tensor(u)
+                if 1 <= u <= ON_TENSOR:
+                    turn_back(u - 1)
+                if u > ON_TENSOR:
+                    second_sum_on_vector(u - 1)
+            first = first + count
+
+        hand_on(0)
+        second_sum_on_vector(UNITS - 1)
+        for u in range(1, UNITS):
+            hand_on(u)
         for q in range(4):
-            nc.scalar.dma_start(
+            (nc.scalar if q < 2 else nc.sync).dma_start(
                 out_2[0, 4 * q : 4 * q + 4, :].bitcast(I32),
                 out_scales[32 * q : 32 * q + 4, :].bitcast(I32),
             )

@@ -19,13 +19,29 @@ SIGMOID = mybir.ActivationFunctionType.Sigmoid
 
 P = 128
 PACK = 4
+QUADRANTS = 4
 UNIT = 128
 UNITS = S // UNIT
 GATHER = 256
 PAD = 8
+Y_BANKS = 4
+
 ROUNDS = (2, 3, 3)
-ON_TENSOR = 5
-WORD_STORES = (5, 8)
+ON_TENSOR = 4
+GPSIMD_SPANS = ((UNIT - 1, 288), (288, 656), (656, S))
+RING = 576
+W2_ON_SCALAR = 96
+W1_ON_SCALAR = 56
+WORD_STORES = (5, UNITS)
+
+AT_WORDS = 0
+AT_RAW1 = 4 * T
+AT_SCALES = AT_RAW1 + 4 * PACK * N
+AT_GATE = AT_SCALES + T
+ROUNDED_BYTES = 2 * UNIT * PACK
+BY_TOKEN_WIDTH = 544
+AT_LAST_BY_TOKEN = ROUNDED_BYTES - 64
+AT_OTHER_BY_TOKEN = (UNITS - ON_TENSOR) * ROUNDED_BYTES
 
 
 def tile_picked_yscan_free_po_kernel(
@@ -34,9 +50,9 @@ def tile_picked_yscan_free_po_kernel(
     nc = tc.nc
     with ExitStack() as ctx:
         keep = ctx.enter_context(tc.tile_pool(name="keep", bufs=1))
-        loads = ctx.enter_context(tc.tile_pool(name="loads", bufs=1))
-        ring = ctx.enter_context(tc.tile_pool(name="ring", bufs=1))
-        psum = ctx.enter_context(tc.psum_pool(name="psum", bufs=4))
+        shared = ctx.enter_context(tc.tile_pool(name="shared", bufs=1))
+        late = ctx.enter_context(tc.tile_pool(name="late", bufs=1))
+        psum = ctx.enter_context(tc.psum_pool(name="psum", bufs=Y_BANKS))
 
         offsets = keep.tile([P, S // 16], U16, name="offsets")
         nc.sync.dma_start(offsets[:], offs)
@@ -44,45 +60,46 @@ def tile_picked_yscan_free_po_kernel(
         raw2 = keep.tile([P, PACK, N], F32, name="raw2", align_bytes=64)
         nc.sync.dma_start(raw2[:], w2.rearrange("(p j) c -> p j c", j=PACK))
 
-        scale_table = loads.tile([P, T], U8, name="scale_table", offset=16384, align_bytes=64)
+        scale_table = shared.tile([P, T], U8, name="scale_table", offset=AT_SCALES, align_bytes=64)
         nc.vector.memset(scale_table[:].bitcast(I32), 0)
-        for q in range(4):
+        for q in range(QUADRANTS):
             nc.sync.dma_start(
                 scale_table[32 * q : 32 * q + 4, :].bitcast(I32),
                 x_scales[0, 4 * q : 4 * q + 4, :].bitcast(I32),
             )
 
-        gate = keep.tile([P, PACK, PAD + S], F32, name="gate", align_bytes=64)
+        gate = shared.tile([P, PACK, PAD + S], F32, name="gate", offset=AT_GATE, align_bytes=64)
         both = keep.tile([P, 2 * PACK, PAD + S], F32, name="both", align_bytes=64)
-        step1 = both[:, 0:PACK, :]
+        ahead = both[:, 0:PACK, :]
         h = both[:, PACK : 2 * PACK, :]
-        zeros = loads.tile([P, T + PACK * N], F32, name="zeros", offset=0, align_bytes=64)
+        zeros = shared.tile([P, T + PACK * N], F32, name="zeros", offset=AT_WORDS, align_bytes=64)
         nc.vector.memset(zeros[:, 0 : 2 * PACK * PAD], 0.0)
         nc.vector.tensor_copy(
             both[:, :, 0:PAD], zeros[:, 0 : 2 * PACK * PAD].rearrange("p (r c) -> p r c", c=PAD)
         )
         nc.scalar.activation(gate[:, :, 0:PAD], h[:, :, 0:PAD], SIGMOID)
 
-        raw1 = loads.tile([P, PACK, N], F32, name="raw1", offset=4 * T, align_bytes=64)
+        raw1 = shared.tile([P, PACK, N], F32, name="raw1", offset=AT_RAW1, align_bytes=64)
         nc.sync.dma_start(raw1[:], w1.rearrange("(p j) c -> p j c", j=PACK))
-        word_table = loads.tile([P, T], I32, name="word_table", offset=0, align_bytes=64)
+        word_table = shared.tile([P, T], I32, name="word_table", offset=AT_WORDS, align_bytes=64)
         nc.sync.dma_start(word_table[:], x_words[0].rearrange("p n r -> p (n r)").bitcast(I32))
 
         identity = keep.tile([P, P], F32, name="identity", align_bytes=64)
         make_identity(nc, identity[:])
 
-        def deal(raw, name, scalar_share):
+        def deal(raw, name, on_scalar):
             grouped = keep.tile([P, PACK, P, PACK], BF16, name=f"grouped{name}", align_bytes=64)
             dealt = grouped[:].rearrange("p t m j -> p m j t")
             source = raw[:].rearrange("p j (m t) -> p m j t", t=PACK)
-            nc.scalar.copy(dealt[:, 0:scalar_share], source[:, 0:scalar_share])
-            if scalar_share < P:
-                nc.vector.tensor_copy(dealt[:, scalar_share:P], source[:, scalar_share:P])
+            nc.scalar.copy(dealt[:, 0:on_scalar], source[:, 0:on_scalar])
+            nc.vector.tensor_copy(dealt[:, on_scalar:P], source[:, on_scalar:P])
             return grouped
 
         def quantise(grouped, name, place):
             codes = keep.tile([P, N], U32, name=f"w_codes{name}", align_bytes=64)
-            scales = loads.tile([P, N], U8, name=f"w_scales{name}", offset=16384 + place * N, align_bytes=64)
+            scales = shared.tile(
+                [P, N], U8, name=f"w_scales{name}", offset=AT_SCALES + place * N, align_bytes=64
+            )
             nc.vector.quantize_mx(
                 out=codes[:].bitcast(FP8X4),
                 scales=scales[:],
@@ -90,18 +107,18 @@ def tile_picked_yscan_free_po_kernel(
             )
             return codes, scales
 
-        grouped2 = deal(raw2, "2", P)
+        grouped2 = deal(raw2, "2", W2_ON_SCALAR)
         x_bytes = keep.tile([P, S], U8, name="x_bytes", align_bytes=64)
         nc.vector.tensor_copy(x_bytes[:], scale_table[:].indirect(offsets[:]))
-        q2 = quantise(grouped2, "2", 0)
-        q1 = quantise(deal(raw1, "1", P // 2), "1", 1)
+        gate_weights = quantise(grouped2, "2", 0)
+        y_weights = quantise(deal(raw1, "1", W1_ON_SCALAR), "1", 1)
 
         x_codes = []
         for c in range(S // GATHER):
             picked = offsets[:, c * GATHER // 16 : (c + 1) * GATHER // 16]
-            codes = keep.tile([P, GATHER], U32, name=f"x_codes{c}", align_bytes=64)
-            nc.vector.tensor_copy(codes[:], word_table[:].bitcast(U32).indirect(picked))
-            x_codes.append(codes)
+            gathered = keep.tile([P, GATHER], U32, name=f"x_codes{c}", align_bytes=64)
+            nc.vector.tensor_copy(gathered[:], word_table[:].bitcast(U32).indirect(picked))
+            x_codes.append(gathered)
 
         def product(weights, u, tag):
             codes, scales = weights
@@ -119,48 +136,44 @@ def tile_picked_yscan_free_po_kernel(
                 )
             return acc
 
-        y = {}
+        y, far, by_token, rounded = {}, {}, {}, {}
 
         def gates(u):
-            acc = product(q2, u, "stage")
+            acc = product(gate_weights, u, "stage")
             nc.scalar.activation(gate[:, :, PAD + u * UNIT : PAD + (u + 1) * UNIT], acc[:], SIGMOID)
 
-        def first_product(u):
+        def near_product(u):
             lo = u * UNIT
             n = min(UNIT, S - 1 - lo)
             nc.vector.tensor_tensor(
-                step1[:, :, PAD + lo : PAD + lo + n],
+                ahead[:, :, PAD + lo : PAD + lo + n],
                 gate[:, :, PAD + lo + 1 : PAD + lo + 1 + n],
                 y[u][:, :, 0:n],
                 MULT,
             )
 
-        def first_sum(u):
+        def near_sum(u):
             lo = u * UNIT
             nc.vector.tensor_tensor(
                 h[:, :, PAD + lo : PAD + lo + UNIT],
-                step1[:, :, PAD + lo - 1 : PAD + lo + UNIT - 1],
+                ahead[:, :, PAD + lo - 1 : PAD + lo + UNIT - 1],
                 y[u][:],
                 ADD,
             )
 
-        out_words = loads.tile([P, S], U32, name="out_words", offset=0, align_bytes=64)
+        out_words = shared.tile([P, S], U32, name="out_words", offset=AT_WORDS, align_bytes=64)
         out_scales = keep.tile([P, S], U8, name="out_scales", align_bytes=64)
         out_rows = out_0.rearrange("(p t) s -> p t s", t=PACK)
         words_hbm = out_1[0].rearrange("p n r -> p (n r)").bitcast(I32)
-        step2, rounded, sums = {}, {}, {}
 
-        def second_product(u, rr, first):
+        def far_product(u):
             lo = u * UNIT
-            step2[u] = keep.tile([P, PACK, UNIT], F32, name=f"step2_{u}", align_bytes=64)
+            far[u] = keep.tile([P, PACK, UNIT], F32, name=f"far{u}", align_bytes=64)
             nc.vector.tensor_tensor(
-                step2[u][:],
-                rr[:, :, (u - first) * UNIT : (u - first + 1) * UNIT],
-                h[:, :, PAD + lo - 2 : PAD + lo - 2 + UNIT],
-                MULT,
+                far[u][:], rr(lo, lo + UNIT), h[:, :, PAD + lo - 2 : PAD + lo - 2 + UNIT], MULT
             )
 
-        def second_sum_on_tensor(u):
+        def far_sum_on_tensor(u):
             lo = u * UNIT
             turned = psum.tile([P, PACK, P], F32, name="stage")
             for t in range(PACK):
@@ -169,35 +182,38 @@ def tile_picked_yscan_free_po_kernel(
                     start=True, stop=False, is_transpose=True,
                 )
                 nc.tensor.matmul(
-                    turned[:, t, :], step2[u][:, t, :], identity[:],
+                    turned[:, t, :], far[u][:, t, :], identity[:],
                     start=False, stop=True, is_transpose=True,
                 )
-            by_token = ring.tile(
-                [P, PACK, P], F32, name=f"by_token{u}", align_bytes=64,
-                offset=512 if (ON_TENSOR - 1 - u) % 2 == 0 else 4096,
+            padded = late.tile(
+                [P, BY_TOKEN_WIDTH], F32, name=f"by_token{u}", align_bytes=64,
+                offset=AT_LAST_BY_TOKEN if (ON_TENSOR - 1 - u) % 2 == 0 else AT_OTHER_BY_TOKEN,
             )
-            nc.scalar.copy(by_token[:], turned[:])
-            sums[u] = by_token
+            by_token[u] = padded[:, 0 : PACK * P].rearrange("p (t m) -> p t m", t=PACK)
+            nc.scalar.copy(by_token[u], turned[:])
 
         def turn_back(u):
             lo = u * UNIT
-            by_token = sums[u]
             back = psum.tile([P, PACK, UNIT], F32, name="stage")
             for t in range(PACK):
-                nc.tensor.transpose(back[:, t, :], by_token[:, t, :], identity[:])
+                nc.tensor.transpose(back[:, t, :], by_token[u][:, t, :], identity[:])
             result = keep.tile([P, PACK, UNIT], F32, name=f"result{u}", align_bytes=64)
             nc.scalar.copy(result[:], back[:])
             nc.sync.dma_start(out_rows[:, :, lo : lo + UNIT], result[:])
             rounded[u] = keep.tile([P, UNIT, PACK], BF16, name=f"rounded{u}", align_bytes=64)
             nc.scalar.copy(rounded[u][:], back[:].rearrange("p t n -> p n t"))
 
-        def second_sum_on_vector(u):
+        def far_sum_on_vector(u):
             lo = u * UNIT
-            result = keep.tile([P, PACK, UNIT], F32, name=f"result{u}", align_bytes=64)
-            nc.vector.tensor_tensor(result[:], step2[u][:], h[:, :, PAD + lo : PAD + lo + UNIT], ADD)
+            result = shared.tile(
+                [P, PACK, UNIT], F32, name=f"result{u}", align_bytes=64,
+                offset=AT_GATE + 4 * PACK * UNIT * (u - ON_TENSOR),
+            )
+            nc.vector.tensor_tensor(result[:], far[u][:], h[:, :, PAD + lo : PAD + lo + UNIT], ADD)
             nc.sync.dma_start(out_rows[:, :, lo : lo + UNIT], result[:])
-            rounded[u] = ring.tile(
-                [P, UNIT, PACK], BF16, name=f"rounded{u}", align_bytes=64, offset=1024 * (u - ON_TENSOR)
+            rounded[u] = late.tile(
+                [P, UNIT, PACK], BF16, name=f"rounded{u}", align_bytes=64,
+                offset=ROUNDED_BYTES * (u - ON_TENSOR),
             )
             nc.scalar.copy(
                 rounded[u][:].rearrange("p (c i) t -> p c t i", i=4),
@@ -212,56 +228,58 @@ def tile_picked_yscan_free_po_kernel(
                 in_=rounded[u][:].rearrange("p n t -> p (n t)"),
             )
             if u + 1 in WORD_STORES:
-                before = max(e for e in (0,) + WORD_STORES if e <= u) * UNIT
+                stored = max(done for done in (0,) + WORD_STORES if done <= u) * UNIT
                 nc.sync.dma_start(
-                    words_hbm[:, before : lo + UNIT], out_words[:, before : lo + UNIT].bitcast(I32)
+                    words_hbm[:, stored : lo + UNIT], out_words[:, stored : lo + UNIT].bitcast(I32)
                 )
 
         gates(0)
         for u in range(UNITS):
             if u + 1 < UNITS:
                 gates(u + 1)
-            if u < 4:
-                y[u] = product(q1, u, "y")
+            if u < Y_BANKS:
+                y[u] = product(y_weights, u, "y")
 
-        places = max(count + i for i, count in enumerate(ROUNDS))
-        rr_all = loads.tile([P, PACK, places * UNIT], F32, name="rr_all", offset=0, align_bytes=64)
-        first = 0
-        for count in ROUNDS:
-            units = range(first, first + count)
-            lo = first * UNIT
-            rr = rr_all[:, :, (places - count) * UNIT : places * UNIT]
-            places = places - 1
-            nc.gpsimd.tensor_tensor(
-                rr,
-                gate[:, :, PAD + lo : PAD + lo + count * UNIT],
-                gate[:, :, PAD + lo - 1 : PAD + lo - 1 + count * UNIT],
-                MULT,
+        rr_ring = shared.tile([P, PACK * RING + S], F32, name="rr_ring", offset=AT_WORDS, align_bytes=64)
+
+        def rr(lo, hi):
+            rows = rr_ring[:, lo : lo + PACK * RING].rearrange("p (t r) -> p t r", t=PACK)
+            return rows[:, :, 0 : hi - lo]
+
+        def gate_product(engine, lo, hi):
+            engine.tensor_tensor(
+                rr(lo, hi), gate[:, :, PAD + lo : PAD + hi], gate[:, :, PAD + lo - 1 : PAD + hi - 1], MULT
             )
+
+        gate_product(nc.vector, 0, UNIT)
+        first = 0
+        for count, span in zip(ROUNDS, GPSIMD_SPANS):
+            units = range(first, first + count)
+            gate_product(nc.gpsimd, *span)
             for u in units:
-                first_product(u)
+                near_product(u)
                 if u > first:
-                    first_sum(u - 1)
-            first_sum(units[-1])
+                    near_sum(u - 1)
+            near_sum(units[-1])
             for u in units:
-                if u + 4 < UNITS:
-                    y[u + 4] = product(q1, u + 4, "y")
+                if u + Y_BANKS < UNITS:
+                    y[u + Y_BANKS] = product(y_weights, u + Y_BANKS, "y")
             for u in units:
-                second_product(u, rr, first)
+                far_product(u)
                 if u < ON_TENSOR:
-                    second_sum_on_tensor(u)
+                    far_sum_on_tensor(u)
                 if 1 <= u <= ON_TENSOR:
                     turn_back(u - 1)
                 if u > ON_TENSOR:
-                    second_sum_on_vector(u - 1)
+                    far_sum_on_vector(u - 1)
             first = first + count
 
         hand_on(0)
-        second_sum_on_vector(UNITS - 1)
+        far_sum_on_vector(UNITS - 1)
         for u in range(1, UNITS):
             hand_on(u)
-        for q in range(4):
-            (nc.scalar if q < 2 else nc.sync).dma_start(
+        for q in range(QUADRANTS):
+            (nc.scalar if q < QUADRANTS // 2 else nc.sync).dma_start(
                 out_2[0, 4 * q : 4 * q + 4, :].bitcast(I32),
                 out_scales[32 * q : 32 * q + 4, :].bitcast(I32),
             )

from contextlib import ExitStack

import concourse.mybir as mybir
from concourse.masks import make_identity

K, T, S, N = 512, 2048, 1024, 512
FLOPS = 2 * 2 * K * N * S

F32 = mybir.dt.float32
BF16 = mybir.dt.bfloat16
I32 = mybir.dt.int32
U32 = mybir.dt.uint32
U16 = mybir.dt.uint16
U8 = mybir.dt.uint8
FP8X4 = mybir.dt.float8_e4m3fn_x4
MULT = mybir.AluOpType.mult
ADD = mybir.AluOpType.add
SIGMOID = mybir.ActivationFunctionType.Sigmoid

P = 128
PACK = 4
QUADRANTS = 4
UNIT = 128
UNITS = S // UNIT
GATHER = 256
PAD = 8
Y_BANKS = 4

ROUNDS = (2, 3, 3)
ON_TENSOR = 4
GPSIMD_SPANS = ((UNIT - 1, 288), (288, 656), (656, S))
RING = 576
W2_ON_SCALAR = 96
W1_ON_SCALAR = 56
WORD_STORES = (5, UNITS)

AT_WORDS = 0
AT_RAW1 = 4 * T
AT_SCALES = AT_RAW1 + 4 * PACK * N
AT_GATE = AT_SCALES + T
ROUNDED_BYTES = 2 * UNIT * PACK
BY_TOKEN_WIDTH = 544
AT_LAST_BY_TOKEN = ROUNDED_BYTES - 64
AT_OTHER_BY_TOKEN = (UNITS - ON_TENSOR) * ROUNDED_BYTES


def tile_picked_yscan_free_po_kernel(
    tc, x_words, x_scales, w1, w2, offs, out_0, out_1, out_2
):
    nc = tc.nc
    with ExitStack() as ctx:
        keep = ctx.enter_context(tc.tile_pool(name="keep", bufs=1))
        shared = ctx.enter_context(tc.tile_pool(name="shared", bufs=1))
        late = ctx.enter_context(tc.tile_pool(name="late", bufs=1))
        psum = ctx.enter_context(tc.psum_pool(name="psum", bufs=Y_BANKS))

        offsets = keep.tile([P, S // 16], U16, name="offsets")
        nc.sync.dma_start(offsets[:], offs)

        raw2 = keep.tile([P, PACK, N], F32, name="raw2", align_bytes=64)
        nc.sync.dma_start(raw2[:], w2.rearrange("(p j) c -> p j c", j=PACK))

        scale_table = shared.tile([P, T], U8, name="scale_table", offset=AT_SCALES, align_bytes=64)
        nc.vector.memset(scale_table[:].bitcast(I32), 0)
        for q in range(QUADRANTS):
            nc.sync.dma_start(
                scale_table[32 * q : 32 * q + 4, :].bitcast(I32),
                x_scales[0, 4 * q : 4 * q + 4, :].bitcast(I32),
            )

        gate = shared.tile([P, PACK, PAD + S], F32, name="gate", offset=AT_GATE, align_bytes=64)
        both = keep.tile([P, 2 * PACK, PAD + S], F32, name="both", align_bytes=64)
        ahead = both[:, 0:PACK, :]
        h = both[:, PACK : 2 * PACK, :]
        zeros = shared.tile([P, T + PACK * N], F32, name="zeros", offset=AT_WORDS, align_bytes=64)
        nc.vector.memset(zeros[:, 0 : 2 * PACK * PAD], 0.0)
        nc.vector.tensor_copy(
            both[:, :, 0:PAD], zeros[:, 0 : 2 * PACK * PAD].rearrange("p (r c) -> p r c", c=PAD)
        )
        nc.scalar.activation(gate[:, :, 0:PAD], h[:, :, 0:PAD], SIGMOID)

        raw1 = shared.tile([P, PACK, N], F32, name="raw1", offset=AT_RAW1, align_bytes=64)
        nc.sync.dma_start(raw1[:], w1.rearrange("(p j) c -> p j c", j=PACK))
        word_table = shared.tile([P, T], I32, name="word_table", offset=AT_WORDS, align_bytes=64)
        nc.sync.dma_start(word_table[:], x_words[0].rearrange("p n r -> p (n r)").bitcast(I32))

        identity = keep.tile([P, P], F32, name="identity", align_bytes=64)
        make_identity(nc, identity[:])

        def deal(raw, name, on_scalar):
            grouped = keep.tile([P, PACK, P, PACK], BF16, name=f"grouped{name}", align_bytes=64)
            dealt = grouped[:].rearrange("p t m j -> p m j t")
            source = raw[:].rearrange("p j (m t) -> p m j t", t=PACK)
            nc.scalar.copy(dealt[:, 0:on_scalar], source[:, 0:on_scalar])
            nc.vector.tensor_copy(dealt[:, on_scalar:P], source[:, on_scalar:P])
            return grouped

        def quantise(grouped, name, place):
            codes = keep.tile([P, N], U32, name=f"w_codes{name}", align_bytes=64)
            scales = shared.tile(
                [P, N], U8, name=f"w_scales{name}", offset=AT_SCALES + place * N, align_bytes=64
            )
            nc.vector.quantize_mx(
                out=codes[:].bitcast(FP8X4),
                scales=scales[:],
                in_=grouped[:].rearrange("p t m j -> p (t m j)"),
            )
            return codes, scales

        grouped2 = deal(raw2, "2", W2_ON_SCALAR)
        x_bytes = keep.tile([P, S], U8, name="x_bytes", align_bytes=64)
        nc.vector.tensor_copy(x_bytes[:], scale_table[:].indirect(offsets[:]))
        gate_weights = quantise(grouped2, "2", 0)
        y_weights = quantise(deal(raw1, "1", W1_ON_SCALAR), "1", 1)

        x_codes = []
        for c in range(S // GATHER):
            picked = offsets[:, c * GATHER // 16 : (c + 1) * GATHER // 16]
            gathered = keep.tile([P, GATHER], U32, name=f"x_codes{c}", align_bytes=64)
            nc.vector.tensor_copy(gathered[:], word_table[:].bitcast(U32).indirect(picked))
            x_codes.append(gathered)

        def product(weights, u, tag):
            codes, scales = weights
            acc = psum.tile([P, PACK, UNIT], F32, name=tag)
            c, lo = divmod(u * UNIT, GATHER)
            for t in range(PACK):
                nc.tensor.matmul_mx(
                    out=acc[:, t, :],
                    lhsT=codes[:, t * P : (t + 1) * P].bitcast(FP8X4),
                    lhsT_scale=scales[:, t * P : (t + 1) * P],
                    rhs=x_codes[c][:, lo : lo + UNIT].bitcast(FP8X4),
                    rhs_scale=x_bytes[:, u * UNIT : (u + 1) * UNIT],
                    start=True,
                    stop=True,
                )
            return acc

        y, far, by_token, rounded = {}, {}, {}, {}

        def gates(u):
            acc = product(gate_weights, u, "stage")
            nc.scalar.activation(gate[:, :, PAD + u * UNIT : PAD + (u + 1) * UNIT], acc[:], SIGMOID)

        def near_product(u):
            lo = u * UNIT
            n = min(UNIT, S - 1 - lo)
            nc.vector.tensor_tensor(
                ahead[:, :, PAD + lo : PAD + lo + n],
                gate[:, :, PAD + lo + 1 : PAD + lo + 1 + n],
                y[u][:, :, 0:n],
                MULT,
            )

        def near_sum(u):
            lo = u * UNIT
            nc.vector.tensor_tensor(
                h[:, :, PAD + lo : PAD + lo + UNIT],
                ahead[:, :, PAD + lo - 1 : PAD + lo + UNIT - 1],
                y[u][:],
                ADD,
            )

        out_words = shared.tile([P, S], U32, name="out_words", offset=AT_WORDS, align_bytes=64)
        out_scales = keep.tile([P, S], U8, name="out_scales", align_bytes=64)
        out_rows = out_0.rearrange("(p t) s -> p t s", t=PACK)
        words_hbm = out_1[0].rearrange("p n r -> p (n r)").bitcast(I32)

        def far_product(u):
            lo = u * UNIT
            far[u] = keep.tile([P, PACK, UNIT], F32, name=f"far{u}", align_bytes=64)
            nc.vector.tensor_tensor(
                far[u][:], rr(lo, lo + UNIT), h[:, :, PAD + lo - 2 : PAD + lo - 2 + UNIT], MULT
            )

        def far_sum_on_tensor(u):
            lo = u * UNIT
            turned = psum.tile([P, PACK, P], F32, name="stage")
            for t in range(PACK):
                nc.tensor.matmul(
                    turned[:, t, :], h[:, t, PAD + lo : PAD + lo + UNIT], identity[:],
                    start=True, stop=False, is_transpose=True,
                )
                nc.tensor.matmul(
                    turned[:, t, :], far[u][:, t, :], identity[:],
                    start=False, stop=True, is_transpose=True,
                )
            padded = late.tile(
                [P, BY_TOKEN_WIDTH], F32, name=f"by_token{u}", align_bytes=64,
                offset=AT_LAST_BY_TOKEN if (ON_TENSOR - 1 - u) % 2 == 0 else AT_OTHER_BY_TOKEN,
            )
            by_token[u] = padded[:, 0 : PACK * P].rearrange("p (t m) -> p t m", t=PACK)
            nc.scalar.copy(by_token[u], turned[:])

        def turn_back(u):
            lo = u * UNIT
            back = psum.tile([P, PACK, UNIT], F32, name="stage")
            for t in range(PACK):
                nc.tensor.transpose(back[:, t, :], by_token[u][:, t, :], identity[:])
            result = keep.tile([P, PACK, UNIT], F32, name=f"result{u}", align_bytes=64)
            nc.scalar.copy(result[:], back[:])
            nc.sync.dma_start(out_rows[:, :, lo : lo + UNIT], result[:])
            rounded[u] = keep.tile([P, UNIT, PACK], BF16, name=f"rounded{u}", align_bytes=64)
            nc.scalar.copy(rounded[u][:], back[:].rearrange("p t n -> p n t"))

        def far_sum_on_vector(u):
            lo = u * UNIT
            result = shared.tile(
                [P, PACK, UNIT], F32, name=f"result{u}", align_bytes=64,
                offset=AT_GATE + 4 * PACK * UNIT * (u - ON_TENSOR),
            )
            nc.vector.tensor_tensor(result[:], far[u][:], h[:, :, PAD + lo : PAD + lo + UNIT], ADD)
            nc.sync.dma_start(out_rows[:, :, lo : lo + UNIT], result[:])
            rounded[u] = late.tile(
                [P, UNIT, PACK], BF16, name=f"rounded{u}", align_bytes=64,
                offset=ROUNDED_BYTES * (u - ON_TENSOR),
            )
            nc.scalar.copy(
                rounded[u][:].rearrange("p (c i) t -> p c t i", i=4),
                result[:].rearrange("p t (c i) -> p c t i", i=4),
            )

        def hand_on(u):
            lo = u * UNIT
            nc.vector.quantize_mx(
                out=out_words[:, lo : lo + UNIT].bitcast(FP8X4),
                scales=out_scales[:, lo : lo + UNIT],
                in_=rounded[u][:].rearrange("p n t -> p (n t)"),
            )
            if u + 1 in WORD_STORES:
                stored = max(done for done in (0,) + WORD_STORES if done <= u) * UNIT
                nc.sync.dma_start(
                    words_hbm[:, stored : lo + UNIT], out_words[:, stored : lo + UNIT].bitcast(I32)
                )

        gates(0)
        for u in range(UNITS):
            if u + 1 < UNITS:
                gates(u + 1)
            if u < Y_BANKS:
                y[u] = product(y_weights, u, "y")

        rr_ring = shared.tile([P, PACK * RING + S], F32, name="rr_ring", offset=AT_WORDS, align_bytes=64)

        def rr(lo, hi):
            rows = rr_ring[:, lo : lo + PACK * RING].rearrange("p (t r) -> p t r", t=PACK)
            return rows[:, :, 0 : hi - lo]

        def gate_product(engine, lo, hi):
            engine.tensor_tensor(
                rr(lo, hi), gate[:, :, PAD + lo : PAD + hi], gate[:, :, PAD + lo - 1 : PAD + hi - 1], MULT
            )

        gate_product(nc.vector, 0, UNIT)
        first = 0
        for count, span in zip(ROUNDS, GPSIMD_SPANS):
            units = range(first, first + count)
            gate_product(nc.gpsimd, *span)
            for u in units:
                near_product(u)
                if u > first:
                    near_sum(u - 1)
            near_sum(units[-1])
            for u in units:
                if u + Y_BANKS < UNITS:
                    y[u + Y_BANKS] = product(y_weights, u + Y_BANKS, "y")
            for u in units:
                far_product(u)
                if u < ON_TENSOR:
                    far_sum_on_tensor(u)
                if 1 <= u <= ON_TENSOR:
                    turn_back(u - 1)
                if u > ON_TENSOR:
                    far_sum_on_vector(u - 1)
            first = first + count

        hand_on(0)
        far_sum_on_vector(UNITS - 1)
        for u in range(1, UNITS):
            hand_on(u)
        for q in range(QUADRANTS):
            (nc.scalar if q < QUADRANTS // 2 else nc.sync).dma_start(
                out_2[0, 4 * q : 4 * q + 4, :].bitcast(I32),
                out_scales[32 * q : 32 * q + 4, :].bitcast(I32),
            )
